import numpy as np
import ml_dtypes


def mxq(x, axis, fmt="e4m3"):
    dtype, down = {"e4m3": (ml_dtypes.float8_e4m3fn, 7), "e5m2": (ml_dtypes.float8_e5m2, 14)}[fmt]
    v = np.moveaxis(np.asarray(x, np.float32).astype(ml_dtypes.bfloat16).astype(np.float64), axis, -1)
    blocks = v.reshape(v.shape[:-1] + (-1, 32))
    amax = np.abs(blocks).max(-1, keepdims=True)
    byte = np.maximum(np.where(amax > 0, np.frexp(amax)[1] - 1 + 127, 0) - down, 1)
    scale = np.exp2(byte - 127.0)
    codes = (blocks / scale).astype(np.float32).astype(dtype).astype(np.float64)
    return np.moveaxis((codes * scale).reshape(v.shape), -1, axis)


WIDE = False


def mx_kscale(k):
    if not WIDE:
        return np.ones(k)
    levels = np.array([10, -10, 5, -5, 0])
    if k % 512:
        return np.exp2(np.random.permutation(np.resize(levels, k // 32))).repeat(32)
    a = np.empty((k // 512, 16))
    for p in range(k // 512):
        a[p, :8] = np.random.permutation(np.resize(levels, 8))
        for g in range(8):
            far = levels[np.abs(levels - a[p, g]) >= 10]
            a[p, g + 8] = far[np.random.randint(len(far))]
    return np.exp2(a.ravel()).repeat(32)


def f64(x):
    return np.asarray(x).astype(np.float64)


def striped(idx):
    return np.tile(idx.reshape(-1, 16).T, (8, 1)).astype(np.uint16)


def unstriped(offs):
    return offs[:16].T.reshape(-1).astype(np.int64)


K, T, S, H, N = 512, 2048, 512, 512, 128


def setup_inputs():
    n = np.random.standard_normal
    s = mx_kscale(K)[:, None]
    u = mx_kscale(H)
    return {
        "xT": (n((K, T)) * s).astype(np.float32),
        "w1": (n((K, H)) / np.sqrt(K) / s * u).astype(np.float32),
        "w2": (n((H, N)) / np.sqrt(H) / u[:, None]).astype(np.float32),
        "pe": (0.5 * n((H, T)) * u[:, None]).astype(np.float32),
        "offs": striped(np.random.permutation(T)[:S]),
    }


def reference(xT, w1, w2, pe, offs):
    xq = mxq(f64(xT)[:, unstriped(offs)], 0, "e4m3")
    g = f64(pe)[:, unstriped(offs)]
    h = (mxq(f64(w1), 0, "e4m3").T @ xq) + g
    return mxq(f64(w2), 0, "e4m3").T @ mxq(h, 0, "e4m3")

@@ -1,0 +1,121 @@
+from contextlib import ExitStack
+
+import concourse.mybir as mybir
+
+K, T, S, H, N = 512, 2048, 512, 512, 128
+FLOPS = 2 * K * H * S + 2 * H * N * S
+
+F32 = mybir.dt.float32
+BF16 = mybir.dt.bfloat16
+U32 = mybir.dt.uint32
+U16 = mybir.dt.uint16
+U8 = mybir.dt.uint8
+FP8X4 = mybir.dt.float8_e4m3fn_x4
+ADD = mybir.AluOpType.add
+
+P = 128
+PACK = 4
+CHUNKS = 2
+C = S // CHUNKS
+
+
+def tile_picked_posadd_none_l_kernel(tc, xT, w1, w2, pe, offs, out):
+    nc = tc.nc
+    with ExitStack() as ctx:
+        keep = ctx.enter_context(tc.tile_pool(name="keep", bufs=1))
+        psum = ctx.enter_context(tc.psum_pool(name="psum", bufs=1))
+
+        offsets = keep.tile([P, S // 16], U16, name="offsets")
+        w1_raw = keep.tile([P, PACK, H], F32, name="w1_raw")
+        w2_raw = keep.tile([P, PACK, N], F32, name="w2_raw")
+        x_rows = [keep.tile([P, T], F32, name="x_rows%d" % t) for t in range(PACK)]
+        pe_rows = [keep.tile([P, T], F32, name="pe_rows%d" % t) for t in range(PACK)]
+
+        x_dram = xT.rearrange("(p j) w -> p j w", j=PACK)
+        pe_dram = pe.rearrange("(p j) w -> p j w", j=PACK)
+        nc.sync.dma_start(out=w1_raw[:], in_=w1.rearrange("(p j) c -> p j c", j=PACK))
+        nc.sync.dma_start(offsets[:], offs)
+        for t in range(PACK):
+            nc.sync.dma_start(out=x_rows[t][:], in_=x_dram[:, t, :])
+        for t in range(PACK):
+            nc.sync.dma_start(out=pe_rows[t][:], in_=pe_dram[:, t, :])
+        nc.sync.dma_start(out=w2_raw[:], in_=w2.rearrange("(p j) c -> p j c", j=PACK))
+
+        def quantize(name, grouped, width):
+            codes = keep.tile([P, width], U32, name=name + "_codes", align_bytes=64)
+            scales = keep.tile([P, width], U8, name=name + "_scales", align_bytes=64)
+            nc.vector.quantize_mx(out=codes[:].bitcast(FP8X4), scales=scales[:], in_=grouped)
+            return codes, scales
+
+        w1_grouped = keep.tile([P, H * PACK], BF16, name="w1_grouped", align_bytes=64)
+        nc.scalar.copy(
+            out=w1_grouped[:].rearrange("p (t m j) -> p t m j", t=PACK, j=PACK),
+            in_=w1_raw[:].rearrange("p j (m t) -> p t m j", t=PACK),
+        )
+        w1_codes, w1_scales = quantize("w1", w1_grouped[:], H)
+
+        x_grouped = keep.tile([P, S, PACK], BF16, name="x_grouped", align_bytes=64)
+        for t in range(PACK):
+            nc.vector.tensor_copy(x_grouped[:, :, t], x_rows[t][:].indirect(offsets[:]))
+        x_codes, x_scales = quantize("x", x_grouped[:].rearrange("p s j -> p (s j)"), S)
+
+        products = []
+        for t in range(PACK):
+            cols = slice(t * P, (t + 1) * P)
+            bank = psum.tile([P, S], F32, name="bank%d" % t)
+            nc.tensor.matmul_mx(
+                out=bank[:],
+                lhsT=w1_codes[:, cols].bitcast(FP8X4),
+                lhsT_scale=w1_scales[:, cols],
+                rhs=x_codes[:].bitcast(FP8X4),
+                rhs_scale=x_scales[:],
+                start=True,
+                stop=True,
+            )
+            product = keep.tile([P, S], F32, name="product%d" % t)
+            nc.scalar.copy(out=product[:], in_=bank[:])
+            products.append(product)
+
+        h_low = keep.tile([P, 2, S], F32, name="h_low")
+        h_high = [keep.tile([P, 2, C], F32, name="h_high%d" % c) for c in range(CHUNKS)]
+        h_grouped = [keep.tile([P, C, PACK], BF16, name="h_grouped%d" % c, align_bytes=64) for c in range(CHUNKS)]
+        for t in range(2):
+            nc.vector.tensor_tensor(h_low[:, t, :], pe_rows[t][:].indirect(offsets[:]), products[t][:], ADD)
+        for c in range(CHUNKS):
+            nc.scalar.copy(
+                out=h_grouped[c][:, :, 0:2],
+                in_=h_low[:, :, c * C : (c + 1) * C].rearrange("p t s -> p s t"),
+            )
+        for t in range(2, PACK):
+            for c in range(CHUNKS):
+                nc.vector.tensor_tensor(
+                    h_high[c][:, t - 2, :],
+                    pe_rows[t][:].indirect(offsets[:, c * C // 16 : (c + 1) * C // 16]),
+                    products[t][:, c * C : (c + 1) * C],
+                    ADD,
+                )
+
+        w2_grouped = keep.tile([P, N, PACK], BF16, name="w2_grouped", align_bytes=64)
+        nc.scalar.copy(out=w2_grouped[:], in_=w2_raw[:].rearrange("p j n -> p n j"))
+        nc.scalar.copy(out=h_grouped[0][:, :, 2:4], in_=h_high[0][:].rearrange("p t s -> p s t"))
+        w2_codes, w2_scales = quantize("w2", w2_grouped[:].rearrange("p n j -> p (n j)"), N)
+        nc.vector.tensor_copy(out=h_grouped[1][:, :, 2:4], in_=h_high[1][:].rearrange("p t s -> p s t"))
+
+        h_q = [quantize("h%d" % c, h_grouped[c][:].rearrange("p s j -> p (s j)"), C) for c in range(CHUNKS)]
+        for c in range(CHUNKS):
+            bank = psum.tile([P, C], F32, name="out_bank%d" % c)
+            nc.tensor.matmul_mx(
+                out=bank[:],
+                lhsT=w2_codes[:].bitcast(FP8X4),
+                lhsT_scale=w2_scales[:],
+                rhs=h_q[c][0][:].bitcast(FP8X4),
+                rhs_scale=h_q[c][1][:],
+                start=True,
+                stop=True,
+            )
+            result = keep.tile([P, C], F32, name="result%d" % c)
+            if c == 0:
+                nc.scalar.copy(out=result[:], in_=bank[:])
+            else:
+                nc.vector.tensor_copy(out=result[:], in_=bank[:])
+            nc.sync.dma_start(out=out[:, c * C : (c + 1) * C], in_=result[:])

@@ -15,8 +15,11 @@ ADD = mybir.AluOpType.add
 
 P = 128
 PACK = 4
-CHUNKS = 2
-C = S // CHUNKS
+WIDTHS = [128,128,128,128]
+STARTS = [sum(WIDTHS[:c]) for c in range(len(WIDTHS))]
+CHUNKS = len(WIDTHS)
+I_ON_VECTOR = [3]
+OUT_ON_VECTOR = []
 
 
 def tile_picked_posadd_none_l_kernel(tc, xT, w1, w2, pe, offs, out):
@@ -59,7 +62,8 @@ def tile_picked_posadd_none_l_kernel(tc, xT, w1, w2, pe, offs, out):
             nc.vector.tensor_copy(x_grouped[:, :, t], x_rows[t][:].indirect(offsets[:]))
         x_codes, x_scales = quantize("x", x_grouped[:].rearrange("p s j -> p (s j)"), S)
 
-        products = []
+        banks = []
+        products = {}
         for t in range(PACK):
             cols = slice(t * P, (t + 1) * P)
             bank = psum.tile([P, S], F32, name="bank%d" % t)
@@ -72,38 +76,39 @@ def tile_picked_posadd_none_l_kernel(tc, xT, w1, w2, pe, offs, out):
                 start=True,
                 stop=True,
             )
-            product = keep.tile([P, S], F32, name="product%d" % t)
-            nc.scalar.copy(out=product[:], in_=bank[:])
-            products.append(product)
+            banks.append(bank)
+            if t > 0:
+                product = keep.tile([P, S], F32, name="product%d" % t)
+                nc.scalar.copy(out=product[:], in_=bank[:])
+                products[t] = product
 
+        spans = [slice(STARTS[c], STARTS[c] + WIDTHS[c]) for c in range(CHUNKS)]
+        lists = [offsets[:, STARTS[c] // 16 : (STARTS[c] + WIDTHS[c]) // 16] for c in range(CHUNKS)]
         h_low = keep.tile([P, 2, S], F32, name="h_low")
-        h_high = [keep.tile([P, 2, C], F32, name="h_high%d" % c) for c in range(CHUNKS)]
-        h_grouped = [keep.tile([P, C, PACK], BF16, name="h_grouped%d" % c, align_bytes=64) for c in range(CHUNKS)]
-        for t in range(2):
-            nc.vector.tensor_tensor(h_low[:, t, :], pe_rows[t][:].indirect(offsets[:]), products[t][:], ADD)
+        h_high = [keep.tile([P, 2, WIDTHS[c]], F32, name="h_high%d" % c) for c in range(CHUNKS)]
+        h_grouped = [keep.tile([P, WIDTHS[c], PACK], BF16, name="h_grouped%d" % c, align_bytes=64) for c in range(CHUNKS)]
+        pe_picked = keep.tile([P, S], F32, name="pe_picked")
+        nc.vector.tensor_copy(pe_picked[:], pe_rows[0][:].indirect(offsets[:]))
+        nc.vector.tensor_tensor(h_low[:, 0, :], banks[0][:], pe_picked[:], ADD)
+        nc.vector.tensor_tensor(h_low[:, 1, :], pe_rows[1][:].indirect(offsets[:]), products[1][:], ADD)
         for c in range(CHUNKS):
-            nc.scalar.copy(
-                out=h_grouped[c][:, :, 0:2],
-                in_=h_low[:, :, c * C : (c + 1) * C].rearrange("p t s -> p s t"),
-            )
+            nc.scalar.copy(out=h_grouped[c][:, :, 0:2], in_=h_low[:, :, spans[c]].rearrange("p t s -> p s t"))
         for t in range(2, PACK):
             for c in range(CHUNKS):
-                nc.vector.tensor_tensor(
-                    h_high[c][:, t - 2, :],
-                    pe_rows[t][:].indirect(offsets[:, c * C // 16 : (c + 1) * C // 16]),
-                    products[t][:, c * C : (c + 1) * C],
-                    ADD,
-                )
-
+                nc.vector.tensor_tensor(h_high[c][:, t - 2, :], pe_rows[t][:].indirect(lists[c]), products[t][:, spans[c]], ADD)
         w2_grouped = keep.tile([P, N, PACK], BF16, name="w2_grouped", align_bytes=64)
-        nc.scalar.copy(out=w2_grouped[:], in_=w2_raw[:].rearrange("p j n -> p n j"))
-        nc.scalar.copy(out=h_grouped[0][:, :, 2:4], in_=h_high[0][:].rearrange("p t s -> p s t"))
-        w2_codes, w2_scales = quantize("w2", w2_grouped[:].rearrange("p n j -> p (n j)"), N)
-        nc.vector.tensor_copy(out=h_grouped[1][:, :, 2:4], in_=h_high[1][:].rearrange("p t s -> p s t"))
+        nc.vector.tensor_copy(out=w2_grouped[:], in_=w2_raw[:].rearrange("p j n -> p n j"))
 
-        h_q = [quantize("h%d" % c, h_grouped[c][:].rearrange("p s j -> p (s j)"), C) for c in range(CHUNKS)]
         for c in range(CHUNKS):
-            bank = psum.tile([P, C], F32, name="out_bank%d" % c)
+            if c in I_ON_VECTOR:
+                nc.vector.tensor_copy(out=h_grouped[c][:, :, 2:4], in_=h_high[c][:].rearrange("p t s -> p s t"))
+            else:
+                nc.scalar.copy(out=h_grouped[c][:, :, 2:4], in_=h_high[c][:].rearrange("p t s -> p s t"))
+
+        w2_codes, w2_scales = quantize("w2", w2_grouped[:].rearrange("p n j -> p (n j)"), N)
+        h_q = [quantize("h%d" % c, h_grouped[c][:].rearrange("p s j -> p (s j)"), WIDTHS[c]) for c in range(CHUNKS)]
+        for c in range(CHUNKS):
+            bank = psum.tile([P, WIDTHS[c]], F32, name="out_bank%d" % c)
             nc.tensor.matmul_mx(
                 out=bank[:],
                 lhsT=w2_codes[:].bitcast(FP8X4),
@@ -113,9 +118,10 @@ def tile_picked_posadd_none_l_kernel(tc, xT, w1, w2, pe, offs, out):
                 start=True,
                 stop=True,
             )
-            result = keep.tile([P, C], F32, name="result%d" % c)
-            if c == 0:
-                nc.scalar.copy(out=result[:], in_=bank[:])
-            else:
+            result = keep.tile([P, WIDTHS[c]], F32, name="result%d" % c)
+            if c in OUT_ON_VECTOR:
                 nc.vector.tensor_copy(out=result[:], in_=bank[:])
-            nc.sync.dma_start(out=out[:, c * C : (c + 1) * C], in_=result[:])
+            else:
+                nc.scalar.copy(out=result[:], in_=bank[:])
+            queue = nc.scalar if c == CHUNKS - 1 else nc.sync
+            queue.dma_start(out=out[:, spans[c]], in_=result[:])

@@ -15,11 +15,10 @@ ADD = mybir.AluOpType.add
 
 P = 128
 PACK = 4
-WIDTHS = [128,128,128,128]
+WIDTHS = [64,128,128,128,64]
 STARTS = [sum(WIDTHS[:c]) for c in range(len(WIDTHS))]
 CHUNKS = len(WIDTHS)
-I_ON_VECTOR = [3]
-OUT_ON_VECTOR = []
+I_ON_VECTOR = [4]
 
 
 def tile_picked_posadd_none_l_kernel(tc, xT, w1, w2, pe, offs, out):
@@ -33,7 +32,8 @@ def tile_picked_posadd_none_l_kernel(tc, xT, w1, w2, pe, offs, out):
         w2_raw = keep.tile([P, PACK, N], F32, name="w2_raw")
         x_rows = [keep.tile([P, T], F32, name="x_rows%d" % t) for t in range(PACK)]
         pe_rows = [keep.tile([P, T], F32, name="pe_rows%d" % t) for t in range(PACK)]
-
+        x_windows = [x_rows[t][:] for t in range(PACK)]
+        pe_windows = [pe_rows[t][:] for t in range(PACK)]
         x_dram = xT.rearrange("(p j) w -> p j w", j=PACK)
         pe_dram = pe.rearrange("(p j) w -> p j w", j=PACK)
         nc.sync.dma_start(out=w1_raw[:], in_=w1.rearrange("(p j) c -> p j c", j=PACK))
@@ -52,18 +52,18 @@ def tile_picked_posadd_none_l_kernel(tc, xT, w1, w2, pe, offs, out):
 
         w1_grouped = keep.tile([P, H * PACK], BF16, name="w1_grouped", align_bytes=64)
         nc.scalar.copy(
-            out=w1_grouped[:].rearrange("p (t m j) -> p t m j", t=PACK, j=PACK),
-            in_=w1_raw[:].rearrange("p j (m t) -> p t m j", t=PACK),
+            out=w1_grouped[:].rearrange("p (t m j) -> p m t j", t=PACK, j=PACK),
+            in_=w1_raw[:].rearrange("p j (m t) -> p m t j", t=PACK),
         )
         w1_codes, w1_scales = quantize("w1", w1_grouped[:], H)
 
         x_grouped = keep.tile([P, S, PACK], BF16, name="x_grouped", align_bytes=64)
         for t in range(PACK):
-            nc.vector.tensor_copy(x_grouped[:, :, t], x_rows[t][:].indirect(offsets[:]))
+            nc.vector.tensor_copy(x_grouped[:, :, t], x_windows[t].indirect(offsets[:]))
         x_codes, x_scales = quantize("x", x_grouped[:].rearrange("p s j -> p (s j)"), S)
 
         banks = []
-        products = {}
+        products = []
         for t in range(PACK):
             cols = slice(t * P, (t + 1) * P)
             bank = psum.tile([P, S], F32, name="bank%d" % t)
@@ -77,27 +77,32 @@ def tile_picked_posadd_none_l_kernel(tc, xT, w1, w2, pe, offs, out):
                 stop=True,
             )
             banks.append(bank)
-            if t > 0:
-                product = keep.tile([P, S], F32, name="product%d" % t)
+            product = keep.tile([P, S], F32, name="product%d" % t)
+            if t not in [0]:
                 nc.scalar.copy(out=product[:], in_=bank[:])
-                products[t] = product
+            products.append(product)
 
         spans = [slice(STARTS[c], STARTS[c] + WIDTHS[c]) for c in range(CHUNKS)]
         lists = [offsets[:, STARTS[c] // 16 : (STARTS[c] + WIDTHS[c]) // 16] for c in range(CHUNKS)]
-        h_low = keep.tile([P, 2, S], F32, name="h_low")
         h_high = [keep.tile([P, 2, WIDTHS[c]], F32, name="h_high%d" % c) for c in range(CHUNKS)]
         h_grouped = [keep.tile([P, WIDTHS[c], PACK], BF16, name="h_grouped%d" % c, align_bytes=64) for c in range(CHUNKS)]
-        pe_picked = keep.tile([P, S], F32, name="pe_picked")
-        nc.vector.tensor_copy(pe_picked[:], pe_rows[0][:].indirect(offsets[:]))
-        nc.vector.tensor_tensor(h_low[:, 0, :], banks[0][:], pe_picked[:], ADD)
-        nc.vector.tensor_tensor(h_low[:, 1, :], pe_rows[1][:].indirect(offsets[:]), products[1][:], ADD)
-        for c in range(CHUNKS):
-            nc.scalar.copy(out=h_grouped[c][:, :, 0:2], in_=h_low[:, :, spans[c]].rearrange("p t s -> p s t"))
+        nc.vector.tensor_copy(products[0][:], pe_windows[0].indirect(offsets[:]))
+        for g, group in enumerate([[0,1],[2],[3,4]]):
+            lo, hi = STARTS[group[0]], STARTS[group[-1]] + WIDTHS[group[-1]]
+            h_low = keep.tile([P, 2, hi - lo], F32, name="h_low%d" % g)
+            nc.vector.tensor_tensor(h_low[:, 0, :], banks[0][:, lo:hi], products[0][:, lo:hi], ADD)
+            nc.vector.tensor_tensor(h_low[:, 1, :], pe_windows[1].indirect(offsets[:, lo // 16 : hi // 16]), products[1][:, lo:hi], ADD)
+            for c in group:
+                part = h_low[:, :, STARTS[c] - lo : STARTS[c] - lo + WIDTHS[c]]
+                nc.scalar.copy(out=h_grouped[c][:, :, 0:2], in_=part.rearrange("p t s -> p s t"))
         for t in range(2, PACK):
             for c in range(CHUNKS):
-                nc.vector.tensor_tensor(h_high[c][:, t - 2, :], pe_rows[t][:].indirect(lists[c]), products[t][:, spans[c]], ADD)
+                nc.vector.tensor_tensor(h_high[c][:, t - 2, :], pe_windows[t].indirect(lists[c]), products[t][:, spans[c]], ADD)
         w2_grouped = keep.tile([P, N, PACK], BF16, name="w2_grouped", align_bytes=64)
-        nc.vector.tensor_copy(out=w2_grouped[:], in_=w2_raw[:].rearrange("p j n -> p n j"))
+        nc.vector.tensor_copy(
+            out=w2_grouped[:].rearrange("p (c i) j -> p c j i", i=4),
+            in_=w2_raw[:].rearrange("p j (c i) -> p c j i", i=4),
+        )
 
         for c in range(CHUNKS):
             if c in I_ON_VECTOR:
@@ -105,10 +110,14 @@ def tile_picked_posadd_none_l_kernel(tc, xT, w1, w2, pe, offs, out):
             else:
                 nc.scalar.copy(out=h_grouped[c][:, :, 2:4], in_=h_high[c][:].rearrange("p t s -> p s t"))
 
-        w2_codes, w2_scales = quantize("w2", w2_grouped[:].rearrange("p n j -> p (n j)"), N)
-        h_q = [quantize("h%d" % c, h_grouped[c][:].rearrange("p s j -> p (s j)"), WIDTHS[c]) for c in range(CHUNKS)]
-        for c in range(CHUNKS):
-            bank = psum.tile([P, WIDTHS[c]], F32, name="out_bank%d" % c)
+        order = [0,1,2,3,4]
+        h_q = {}
+        for c in order:
+            h_q[c] = quantize("h%d" % c, h_grouped[c][:].rearrange("p s j -> p (s j)"), WIDTHS[c])
+            if c == order[0]:
+                w2_codes, w2_scales = quantize("w2", w2_grouped[:].rearrange("p n j -> p (n j)"), N)
+        for c in order:
+            bank = psum.tile([P, WIDTHS[c]], F32, name="out_bank%d" % c, tag="out_bank%d" % c if c < 4 else "bank%d" % (c - 4))
             nc.tensor.matmul_mx(
                 out=bank[:],
                 lhsT=w2_codes[:].bitcast(FP8X4),
@@ -119,9 +128,6 @@ def tile_picked_posadd_none_l_kernel(tc, xT, w1, w2, pe, offs, out):
                 stop=True,
             )
             result = keep.tile([P, WIDTHS[c]], F32, name="result%d" % c)
-            if c in OUT_ON_VECTOR:
-                nc.vector.tensor_copy(out=result[:], in_=bank[:])
-            else:
-                nc.scalar.copy(out=result[:], in_=bank[:])
-            queue = nc.scalar if c == CHUNKS - 1 else nc.sync
+            nc.scalar.copy(out=result[:], in_=bank[:])
+            queue = nc.scalar if c == order[-1] else nc.sync
             queue.dma_start(out=out[:, spans[c]], in_=result[:])

@@ -15,10 +15,10 @@ ADD = mybir.AluOpType.add
 
 P = 128
 PACK = 4
-WIDTHS = [64,128,128,128,64]
+WIDTHS = [128,128,128,128]
 STARTS = [sum(WIDTHS[:c]) for c in range(len(WIDTHS))]
 CHUNKS = len(WIDTHS)
-I_ON_VECTOR = [4]
+I_ON_VECTOR = []
 
 
 def tile_picked_posadd_none_l_kernel(tc, xT, w1, w2, pe, offs, out):
@@ -84,38 +84,51 @@ def tile_picked_posadd_none_l_kernel(tc, xT, w1, w2, pe, offs, out):
 
         spans = [slice(STARTS[c], STARTS[c] + WIDTHS[c]) for c in range(CHUNKS)]
         lists = [offsets[:, STARTS[c] // 16 : (STARTS[c] + WIDTHS[c]) // 16] for c in range(CHUNKS)]
-        h_high = [keep.tile([P, 2, WIDTHS[c]], F32, name="h_high%d" % c) for c in range(CHUNKS)]
         h_grouped = [keep.tile([P, WIDTHS[c], PACK], BF16, name="h_grouped%d" % c, align_bytes=64) for c in range(CHUNKS)]
         nc.vector.tensor_copy(products[0][:], pe_windows[0].indirect(offsets[:]))
-        for g, group in enumerate([[0,1],[2],[3,4]]):
+        for g, group in enumerate([[0,1],[2,3]]):
             lo, hi = STARTS[group[0]], STARTS[group[-1]] + WIDTHS[group[-1]]
             h_low = keep.tile([P, 2, hi - lo], F32, name="h_low%d" % g)
             nc.vector.tensor_tensor(h_low[:, 0, :], banks[0][:, lo:hi], products[0][:, lo:hi], ADD)
             nc.vector.tensor_tensor(h_low[:, 1, :], pe_windows[1].indirect(offsets[:, lo // 16 : hi // 16]), products[1][:, lo:hi], ADD)
             for c in group:
                 part = h_low[:, :, STARTS[c] - lo : STARTS[c] - lo + WIDTHS[c]]
-                nc.scalar.copy(out=h_grouped[c][:, :, 0:2], in_=part.rearrange("p t s -> p s t"))
-        for t in range(2, PACK):
-            for c in range(CHUNKS):
-                nc.vector.tensor_tensor(h_high[c][:, t - 2, :], pe_windows[t].indirect(lists[c]), products[t][:, spans[c]], ADD)
-        w2_grouped = keep.tile([P, N, PACK], BF16, name="w2_grouped", align_bytes=64)
-        nc.vector.tensor_copy(
-            out=w2_grouped[:].rearrange("p (c i) j -> p c j i", i=4),
-            in_=w2_raw[:].rearrange("p j (c i) -> p c j i", i=4),
-        )
+                low_copy = nc.vector.tensor_copy if c in [2,3] else nc.scalar.copy
+                low_copy(out=h_grouped[c][:, :, 0:2], in_=part.rearrange("p t s -> p s t"))
+
+        def gather_add(t, c, dst):
+            nc.vector.tensor_tensor(dst, pe_windows[t].indirect(lists[c]), products[t][:, spans[c]], ADD)
+
+        def weave(t, c, src):
+            copy = nc.vector.tensor_copy if c in I_ON_VECTOR else nc.scalar.copy
+            copy(out=h_grouped[c][:, :, t], in_=src)
+
+        h_q = {}
+
+        def quantize_h(c):
+            h_q[c] = quantize("h%d" % c, h_grouped[c][:].rearrange("p s j -> p (s j)"), WIDTHS[c])
 
         for c in range(CHUNKS):
-            if c in I_ON_VECTOR:
-                nc.vector.tensor_copy(out=h_grouped[c][:, :, 2:4], in_=h_high[c][:].rearrange("p t s -> p s t"))
-            else:
-                nc.scalar.copy(out=h_grouped[c][:, :, 2:4], in_=h_high[c][:].rearrange("p t s -> p s t"))
-
-        order = [0,1,2,3,4]
-        h_q = {}
-        for c in order:
-            h_q[c] = quantize("h%d" % c, h_grouped[c][:].rearrange("p s j -> p (s j)"), WIDTHS[c])
-            if c == order[0]:
-                w2_codes, w2_scales = quantize("w2", w2_grouped[:].rearrange("p n j -> p (n j)"), N)
+            plane = keep.tile([P, WIDTHS[c]], F32, name="h2_%d" % c)
+            gather_add(2, c, plane[:])
+            weave(2, c, plane[:])
+        last = {c: keep.tile([P, WIDTHS[c]], F32, name="h3_%d" % c)[:] for c in range(4)}
+        w2_grouped = keep.tile([P, N, PACK], BF16, name="w2_grouped", align_bytes=64)
+        gather_add(3, 0, last[0])
+        weave(3, 0, last[0])
+        gather_add(3, 1, last[1])
+        weave(3, 1, last[1])
+        gather_add(3, 2, last[2])
+        weave(3, 2, last[2])
+        gather_add(3, 3, last[3])
+        weave(3, 3, last[3])
+        nc.vector.tensor_copy(out=w2_grouped[:], in_=w2_raw[:].rearrange("p j n -> p n j"))
+        quantize_h(0)
+        w2_codes, w2_scales = quantize("w2", w2_grouped[:].rearrange("p n j -> p (n j)"), N)
+        quantize_h(1)
+        quantize_h(2)
+        quantize_h(3)
+        order = [0,1,2,3]
         for c in order:
             bank = psum.tile([P, WIDTHS[c]], F32, name="out_bank%d" % c, tag="out_bank%d" % c if c < 4 else "bank%d" % (c - 4))
             nc.tensor.matmul_mx(

@@ -28,10 +28,10 @@ def tile_picked_posadd_none_l_kernel(tc, xT, w1, w2, pe, offs, out):
         psum = ctx.enter_context(tc.psum_pool(name="psum", bufs=1))
 
         offsets = keep.tile([P, S // 16], U16, name="offsets")
-        w1_raw = keep.tile([P, PACK, H], F32, name="w1_raw")
-        w2_raw = keep.tile([P, PACK, N], F32, name="w2_raw")
-        x_rows = [keep.tile([P, T], F32, name="x_rows%d" % t) for t in range(PACK)]
-        pe_rows = [keep.tile([P, T], F32, name="pe_rows%d" % t) for t in range(PACK)]
+        w1_raw = keep.tile([P, PACK, H], F32, name="w1_raw", align_bytes=256)
+        w2_raw = keep.tile([P, PACK, N], F32, name="w2_raw", align_bytes=256)
+        x_rows = [keep.tile([P, T], F32, name="x_rows%d" % t, align_bytes=256) for t in range(PACK)]
+        pe_rows = [keep.tile([P, T], F32, name="pe_rows%d" % t, align_bytes=256) for t in range(PACK)]
         x_windows = [x_rows[t][:] for t in range(PACK)]
         pe_windows = [pe_rows[t][:] for t in range(PACK)]
         x_dram = xT.rearrange("(p j) w -> p j w", j=PACK)
@@ -140,7 +140,7 @@ def tile_picked_posadd_none_l_kernel(tc, xT, w1, w2, pe, offs, out):
                 start=True,
                 stop=True,
             )
-            result = keep.tile([P, WIDTHS[c]], F32, name="result%d" % c)
+            result = keep.tile([P, WIDTHS[c]], F32, name="result%d" % c, align_bytes=256)
             nc.scalar.copy(out=result[:], in_=bank[:])
             queue = nc.scalar if c == order[-1] else nc.sync
             queue.dma_start(out=out[:, spans[c]], in_=result[:])

@@ -15,10 +15,9 @@ ADD = mybir.AluOpType.add
 
 P = 128
 PACK = 4
-WIDTHS = [128,128,128,128]
-STARTS = [sum(WIDTHS[:c]) for c in range(len(WIDTHS))]
-CHUNKS = len(WIDTHS)
-I_ON_VECTOR = []
+CHUNK = 128
+CHUNKS = S // CHUNK
+DMA_ALIGN = 256
 
 
 def tile_picked_posadd_none_l_kernel(tc, xT, w1, w2, pe, offs, out):
@@ -27,39 +26,57 @@ def tile_picked_posadd_none_l_kernel(tc, xT, w1, w2, pe, offs, out):
         keep = ctx.enter_context(tc.tile_pool(name="keep", bufs=1))
         psum = ctx.enter_context(tc.psum_pool(name="psum", bufs=1))
 
-        offsets = keep.tile([P, S // 16], U16, name="offsets")
-        w1_raw = keep.tile([P, PACK, H], F32, name="w1_raw", align_bytes=256)
-        w2_raw = keep.tile([P, PACK, N], F32, name="w2_raw", align_bytes=256)
-        x_rows = [keep.tile([P, T], F32, name="x_rows%d" % t, align_bytes=256) for t in range(PACK)]
-        pe_rows = [keep.tile([P, T], F32, name="pe_rows%d" % t, align_bytes=256) for t in range(PACK)]
-        x_windows = [x_rows[t][:] for t in range(PACK)]
-        pe_windows = [pe_rows[t][:] for t in range(PACK)]
-        x_dram = xT.rearrange("(p j) w -> p j w", j=PACK)
-        pe_dram = pe.rearrange("(p j) w -> p j w", j=PACK)
-        nc.sync.dma_start(out=w1_raw[:], in_=w1.rearrange("(p j) c -> p j c", j=PACK))
-        nc.sync.dma_start(offsets[:], offs)
-        for t in range(PACK):
-            nc.sync.dma_start(out=x_rows[t][:], in_=x_dram[:, t, :])
-        for t in range(PACK):
-            nc.sync.dma_start(out=pe_rows[t][:], in_=pe_dram[:, t, :])
-        nc.sync.dma_start(out=w2_raw[:], in_=w2.rearrange("(p j) c -> p j c", j=PACK))
-
         def quantize(name, grouped, width):
             codes = keep.tile([P, width], U32, name=name + "_codes", align_bytes=64)
             scales = keep.tile([P, width], U8, name=name + "_scales", align_bytes=64)
             nc.vector.quantize_mx(out=codes[:].bitcast(FP8X4), scales=scales[:], in_=grouped)
             return codes, scales
 
+        def multiply(bank, stationary, moving):
+            nc.tensor.matmul_mx(
+                out=bank,
+                lhsT=stationary[0].bitcast(FP8X4),
+                lhsT_scale=stationary[1],
+                rhs=moving[0].bitcast(FP8X4),
+                rhs_scale=moving[1],
+                start=True,
+                stop=True,
+            )
+
+        offsets = keep.tile([P, S // 16], U16, name="offsets")
+        w1_raw = keep.tile([P, PACK, H], F32, name="w1_raw", align_bytes=DMA_ALIGN)
+        w2_raw = keep.tile([P, PACK, N], F32, name="w2_raw", align_bytes=DMA_ALIGN)
+        x_early = keep.tile([P, 3, T], F32, name="x_early", align_bytes=DMA_ALIGN)
+        x_late = keep.tile([P, T], F32, name="x_late", align_bytes=DMA_ALIGN)
+        pe_rows = [keep.tile([P, T], F32, name="pe_rows%d" % t, align_bytes=DMA_ALIGN) for t in range(PACK)]
+        x_dram = xT.rearrange("(p j) w -> p j w", j=PACK)
+        pe_dram = pe.rearrange("(p j) w -> p j w", j=PACK)
+        nc.sync.dma_start(out=x_early[:], in_=x_dram[:, 0:3, :])
+        nc.sync.dma_start(offsets[:], offs)
+        nc.sync.dma_start(out=w1_raw[:], in_=w1.rearrange("(p j) c -> p j c", j=PACK))
+        nc.sync.dma_start(out=x_late[:], in_=x_dram[:, 3, :])
+        for t in range(PACK):
+            nc.sync.dma_start(out=pe_rows[t][:], in_=pe_dram[:, t, :])
+        nc.sync.dma_start(out=w2_raw[:], in_=w2.rearrange("(p j) c -> p j c", j=PACK))
+
+        HALF = S // 2
+        x_grouped = keep.tile([P, S, PACK], BF16, name="x_grouped", align_bytes=64)
+        x_picked = [keep.tile([P, 2, HALF], F32, name="x_picked%d" % g) for g in range(2)]
+        halves = [offsets[:, g * HALF // 16 : (g + 1) * HALF // 16] for g in range(2)]
+        for g in range(2):
+            for t in range(2):
+                nc.vector.tensor_copy(x_picked[g][:, t, :], x_early[:, t, :].indirect(halves[g]))
+        nc.vector.tensor_copy(x_grouped[:, :, 2], x_early[:, 2, :].indirect(offsets[:]))
+        nc.vector.tensor_copy(x_grouped[:, :, 3], x_late[:].indirect(offsets[:]))
+        nc.scalar.copy(out=x_grouped[:, :HALF, 0:2], in_=x_picked[0][:].rearrange("p t s -> p s t"))
+
         w1_grouped = keep.tile([P, H * PACK], BF16, name="w1_grouped", align_bytes=64)
         nc.scalar.copy(
             out=w1_grouped[:].rearrange("p (t m j) -> p m t j", t=PACK, j=PACK),
             in_=w1_raw[:].rearrange("p j (m t) -> p m t j", t=PACK),
         )
+        nc.scalar.copy(out=x_grouped[:, HALF:, 0:2], in_=x_picked[1][:].rearrange("p t s -> p s t"))
         w1_codes, w1_scales = quantize("w1", w1_grouped[:], H)
-
-        x_grouped = keep.tile([P, S, PACK], BF16, name="x_grouped", align_bytes=64)
-        for t in range(PACK):
-            nc.vector.tensor_copy(x_grouped[:, :, t], x_windows[t].indirect(offsets[:]))
         x_codes, x_scales = quantize("x", x_grouped[:].rearrange("p s j -> p (s j)"), S)
 
         banks = []
@@ -67,80 +84,42 @@ def tile_picked_posadd_none_l_kernel(tc, xT, w1, w2, pe, offs, out):
         for t in range(PACK):
             cols = slice(t * P, (t + 1) * P)
             bank = psum.tile([P, S], F32, name="bank%d" % t)
-            nc.tensor.matmul_mx(
-                out=bank[:],
-                lhsT=w1_codes[:, cols].bitcast(FP8X4),
-                lhsT_scale=w1_scales[:, cols],
-                rhs=x_codes[:].bitcast(FP8X4),
-                rhs_scale=x_scales[:],
-                start=True,
-                stop=True,
-            )
+            multiply(bank[:], (w1_codes[:, cols], w1_scales[:, cols]), (x_codes[:], x_scales[:]))
             banks.append(bank)
             product = keep.tile([P, S], F32, name="product%d" % t)
-            if t not in [0]:
+            if t > 0:
                 nc.scalar.copy(out=product[:], in_=bank[:])
             products.append(product)
 
-        spans = [slice(STARTS[c], STARTS[c] + WIDTHS[c]) for c in range(CHUNKS)]
-        lists = [offsets[:, STARTS[c] // 16 : (STARTS[c] + WIDTHS[c]) // 16] for c in range(CHUNKS)]
-        h_grouped = [keep.tile([P, WIDTHS[c], PACK], BF16, name="h_grouped%d" % c, align_bytes=64) for c in range(CHUNKS)]
-        nc.vector.tensor_copy(products[0][:], pe_windows[0].indirect(offsets[:]))
-        for g, group in enumerate([[0,1],[2,3]]):
-            lo, hi = STARTS[group[0]], STARTS[group[-1]] + WIDTHS[group[-1]]
-            h_low = keep.tile([P, 2, hi - lo], F32, name="h_low%d" % g)
-            nc.vector.tensor_tensor(h_low[:, 0, :], banks[0][:, lo:hi], products[0][:, lo:hi], ADD)
-            nc.vector.tensor_tensor(h_low[:, 1, :], pe_windows[1].indirect(offsets[:, lo // 16 : hi // 16]), products[1][:, lo:hi], ADD)
-            for c in group:
-                part = h_low[:, :, STARTS[c] - lo : STARTS[c] - lo + WIDTHS[c]]
-                low_copy = nc.vector.tensor_copy if c in [2,3] else nc.scalar.copy
-                low_copy(out=h_grouped[c][:, :, 0:2], in_=part.rearrange("p t s -> p s t"))
+        spans = [slice(c * CHUNK, (c + 1) * CHUNK) for c in range(CHUNKS)]
+        lists = [offsets[:, c * CHUNK // 16 : (c + 1) * CHUNK // 16] for c in range(CHUNKS)]
+        h_grouped = [keep.tile([P, CHUNK, PACK], BF16, name="h_grouped%d" % c, align_bytes=64) for c in range(CHUNKS)]
+        h_sums = keep.tile([P, 3, S], F32, name="h_sums")
+        nc.vector.tensor_copy(products[0][:], pe_rows[0][:].indirect(offsets[:]))
+        nc.vector.tensor_tensor(h_sums[:, 0, :], banks[0][:], products[0][:], ADD)
+        nc.vector.tensor_tensor(h_sums[:, 1, :], pe_rows[1][:].indirect(offsets[:]), products[1][:], ADD)
+        for c in range(CHUNKS):
+            nc.vector.tensor_tensor(h_sums[:, 2, spans[c]], pe_rows[2][:].indirect(lists[c]), products[2][:, spans[c]], ADD)
+            early_copy = nc.vector.tensor_copy if c == CHUNKS - 1 else nc.scalar.copy
+            early_copy(out=h_grouped[c][:, :, 0:3], in_=h_sums[:, :, spans[c]].rearrange("p t s -> p s t"))
 
-        def gather_add(t, c, dst):
-            nc.vector.tensor_tensor(dst, pe_windows[t].indirect(lists[c]), products[t][:, spans[c]], ADD)
-
-        def weave(t, c, src):
-            copy = nc.vector.tensor_copy if c in I_ON_VECTOR else nc.scalar.copy
-            copy(out=h_grouped[c][:, :, t], in_=src)
-
-        h_q = {}
-
-        def quantize_h(c):
-            h_q[c] = quantize("h%d" % c, h_grouped[c][:].rearrange("p s j -> p (s j)"), WIDTHS[c])
+        def gather_add(t, c):
+            plane = keep.tile([P, CHUNK], F32, name="h%d_%d" % (t, c))
+            nc.vector.tensor_tensor(plane[:], pe_rows[t][:].indirect(lists[c]), products[t][:, spans[c]], ADD)
+            return plane
 
         for c in range(CHUNKS):
-            plane = keep.tile([P, WIDTHS[c]], F32, name="h2_%d" % c)
-            gather_add(2, c, plane[:])
-            weave(2, c, plane[:])
-        last = {c: keep.tile([P, WIDTHS[c]], F32, name="h3_%d" % c)[:] for c in range(4)}
+            nc.scalar.copy(out=h_grouped[c][:, :, 3], in_=gather_add(3, c)[:])
         w2_grouped = keep.tile([P, N, PACK], BF16, name="w2_grouped", align_bytes=64)
-        gather_add(3, 0, last[0])
-        weave(3, 0, last[0])
-        gather_add(3, 1, last[1])
-        weave(3, 1, last[1])
-        gather_add(3, 2, last[2])
-        weave(3, 2, last[2])
-        gather_add(3, 3, last[3])
-        weave(3, 3, last[3])
         nc.vector.tensor_copy(out=w2_grouped[:], in_=w2_raw[:].rearrange("p j n -> p n j"))
-        quantize_h(0)
+        h_q = [quantize("h0", h_grouped[0][:].rearrange("p s j -> p (s j)"), CHUNK)]
         w2_codes, w2_scales = quantize("w2", w2_grouped[:].rearrange("p n j -> p (n j)"), N)
-        quantize_h(1)
-        quantize_h(2)
-        quantize_h(3)
-        order = [0,1,2,3]
-        for c in order:
-            bank = psum.tile([P, WIDTHS[c]], F32, name="out_bank%d" % c, tag="out_bank%d" % c if c < 4 else "bank%d" % (c - 4))
-            nc.tensor.matmul_mx(
-                out=bank[:],
-                lhsT=w2_codes[:].bitcast(FP8X4),
-                lhsT_scale=w2_scales[:],
-                rhs=h_q[c][0][:].bitcast(FP8X4),
-                rhs_scale=h_q[c][1][:],
-                start=True,
-                stop=True,
-            )
-            result = keep.tile([P, WIDTHS[c]], F32, name="result%d" % c, align_bytes=256)
+        for c in range(1, CHUNKS):
+            h_q.append(quantize("h%d" % c, h_grouped[c][:].rearrange("p s j -> p (s j)"), CHUNK))
+        for c in range(CHUNKS):
+            bank = psum.tile([P, CHUNK], F32, name="out_bank%d" % c)
+            multiply(bank[:], (w2_codes[:], w2_scales[:]), (h_q[c][0][:], h_q[c][1][:]))
+            result = keep.tile([P, CHUNK], F32, name="result%d" % c, align_bytes=DMA_ALIGN)
             nc.scalar.copy(out=result[:], in_=bank[:])
-            queue = nc.scalar if c == order[-1] else nc.sync
+            queue = nc.scalar if c == CHUNKS - 1 else nc.sync
             queue.dma_start(out=out[:, spans[c]], in_=result[:])

@@ -108,18 +108,24 @@ def tile_picked_posadd_none_l_kernel(tc, xT, w1, w2, pe, offs, out):
             nc.vector.tensor_tensor(plane[:], pe_rows[t][:].indirect(lists[c]), products[t][:, spans[c]], ADD)
             return plane
 
-        for c in range(CHUNKS):
-            nc.scalar.copy(out=h_grouped[c][:, :, 3], in_=gather_add(3, c)[:])
         w2_grouped = keep.tile([P, N, PACK], BF16, name="w2_grouped", align_bytes=64)
+        pieces = [(c, 0, CHUNK) for c in range(CHUNKS - 1)] + [(CHUNKS - 1, 0, CHUNK // 2), (CHUNKS - 1, CHUNK // 2, CHUNK)]
+        last_plane = [gather_add(3, c) for c in range(CHUNKS)]
+        for c, lo, hi in pieces:
+            nc.scalar.copy(out=h_grouped[c][:, lo:hi, 3], in_=last_plane[c][:, lo:hi])
         nc.vector.tensor_copy(out=w2_grouped[:], in_=w2_raw[:].rearrange("p j n -> p n j"))
-        h_q = [quantize("h0", h_grouped[0][:].rearrange("p s j -> p (s j)"), CHUNK)]
+
+        def quantize_h(c, lo, hi):
+            return quantize("h%d_%d" % (c, lo), h_grouped[c][:, lo:hi, :].rearrange("p s j -> p (s j)"), hi - lo)
+
+        h_q = [quantize_h(*pieces[0])]
         w2_codes, w2_scales = quantize("w2", w2_grouped[:].rearrange("p n j -> p (n j)"), N)
-        for c in range(1, CHUNKS):
-            h_q.append(quantize("h%d" % c, h_grouped[c][:].rearrange("p s j -> p (s j)"), CHUNK))
-        for c in range(CHUNKS):
-            bank = psum.tile([P, CHUNK], F32, name="out_bank%d" % c)
-            multiply(bank[:], (w2_codes[:], w2_scales[:]), (h_q[c][0][:], h_q[c][1][:]))
-            result = keep.tile([P, CHUNK], F32, name="result%d" % c, align_bytes=DMA_ALIGN)
+        for piece in pieces[1:]:
+            h_q.append(quantize_h(*piece))
+        for i, (c, lo, hi) in enumerate(pieces):
+            bank = psum.tile([P, hi - lo], F32, name="out_bank%d" % i, tag="out_bank%d" % i if i < CHUNKS else "bank0")
+            multiply(bank[:], (w2_codes[:], w2_scales[:]), (h_q[i][0][:], h_q[i][1][:]))
+            result = keep.tile([P, hi - lo], F32, name="result%d" % i, align_bytes=DMA_ALIGN)
             nc.scalar.copy(out=result[:], in_=bank[:])
-            queue = nc.scalar if c == CHUNKS - 1 else nc.sync
-            queue.dma_start(out=out[:, spans[c]], in_=result[:])
+            queue = nc.scalar if i == len(pieces) - 1 else nc.sync
+            queue.dma_start(out=out[:, c * CHUNK + lo : c * CHUNK + hi], in_=result[:])

@@ -122,10 +122,11 @@ def tile_picked_posadd_none_l_kernel(tc, xT, w1, w2, pe, offs, out):
         w2_codes, w2_scales = quantize("w2", w2_grouped[:].rearrange("p n j -> p (n j)"), N)
         for piece in pieces[1:]:
             h_q.append(quantize_h(*piece))
+        results = [keep.tile([P, CHUNK], F32, name="result%d" % c, align_bytes=DMA_ALIGN) for c in range(CHUNKS)]
         for i, (c, lo, hi) in enumerate(pieces):
             bank = psum.tile([P, hi - lo], F32, name="out_bank%d" % i, tag="out_bank%d" % i if i < CHUNKS else "bank0")
             multiply(bank[:], (w2_codes[:], w2_scales[:]), (h_q[i][0][:], h_q[i][1][:]))
-            result = keep.tile([P, hi - lo], F32, name="result%d" % i, align_bytes=DMA_ALIGN)
-            nc.scalar.copy(out=result[:], in_=bank[:])
-            queue = nc.scalar if i == len(pieces) - 1 else nc.sync
-            queue.dma_start(out=out[:, c * CHUNK + lo : c * CHUNK + hi], in_=result[:])
+            nc.scalar.copy(out=results[c][:, lo:hi], in_=bank[:])
+            if hi == CHUNK:
+                queue = nc.scalar if c == CHUNKS - 1 else nc.sync
+                queue.dma_start(out=out[:, spans[c]], in_=results[c][:])

@@ -67,7 +67,8 @@ def tile_picked_posadd_none_l_kernel(tc, xT, w1, w2, pe, offs, out):
             for t in range(2):
                 nc.vector.tensor_copy(x_picked[g][:, t, :], x_early[:, t, :].indirect(halves[g]))
         nc.vector.tensor_copy(x_grouped[:, :, 2], x_early[:, 2, :].indirect(offsets[:]))
-        nc.vector.tensor_copy(x_grouped[:, :, 3], x_late[:].indirect(offsets[:]))
+        for g in range(2):
+            nc.vector.tensor_copy(x_grouped[:, g * HALF : (g + 1) * HALF, 3], x_late[:].indirect(halves[g]))
         nc.scalar.copy(out=x_grouped[:, :HALF, 0:2], in_=x_picked[0][:].rearrange("p t s -> p s t"))
 
         w1_grouped = keep.tile([P, H * PACK], BF16, name="w1_grouped", align_bytes=64)
@@ -77,19 +78,24 @@ def tile_picked_posadd_none_l_kernel(tc, xT, w1, w2, pe, offs, out):
         )
         nc.scalar.copy(out=x_grouped[:, HALF:, 0:2], in_=x_picked[1][:].rearrange("p t s -> p s t"))
         w1_codes, w1_scales = quantize("w1", w1_grouped[:], H)
-        x_codes, x_scales = quantize("x", x_grouped[:].rearrange("p s j -> p (s j)"), S)
+        x_q = [
+            quantize("x%d" % g, x_grouped[:, g * HALF : (g + 1) * HALF, :].rearrange("p s j -> p (s j)"), HALF)
+            for g in range(2)
+        ]
 
-        banks = []
-        products = []
-        for t in range(PACK):
-            cols = slice(t * P, (t + 1) * P)
-            bank = psum.tile([P, S], F32, name="bank%d" % t)
-            multiply(bank[:], (w1_codes[:, cols], w1_scales[:, cols]), (x_codes[:], x_scales[:]))
-            banks.append(bank)
-            product = keep.tile([P, S], F32, name="product%d" % t)
-            if t > 0:
-                nc.scalar.copy(out=product[:], in_=bank[:])
-            products.append(product)
+        banks = [psum.tile([P, S], F32, name="bank%d" % t) for t in range(PACK)]
+        for planes in ((1, 0), (2, 3)):
+            for g in range(2):
+                for t in planes:
+                    cols = slice(t * P, (t + 1) * P)
+                    multiply(
+                        banks[t][:, g * HALF : (g + 1) * HALF],
+                        (w1_codes[:, cols], w1_scales[:, cols]),
+                        (x_q[g][0][:], x_q[g][1][:]),
+                    )
+        products = [keep.tile([P, S], F32, name="product%d" % t) for t in range(PACK)]
+        for t in range(1, PACK):
+            nc.scalar.copy(out=products[t][:], in_=banks[t][:])
 
         spans = [slice(c * CHUNK, (c + 1) * CHUNK) for c in range(CHUNKS)]
         lists = [offsets[:, c * CHUNK // 16 : (c + 1) * CHUNK // 16] for c in range(CHUNKS)]
@@ -100,7 +106,8 @@ def tile_picked_posadd_none_l_kernel(tc, xT, w1, w2, pe, offs, out):
         nc.vector.tensor_tensor(h_sums[:, 1, :], pe_rows[1][:].indirect(offsets[:]), products[1][:], ADD)
         for c in range(CHUNKS):
             nc.vector.tensor_tensor(h_sums[:, 2, spans[c]], pe_rows[2][:].indirect(lists[c]), products[2][:, spans[c]], ADD)
-            early_copy = nc.vector.tensor_copy if c == CHUNKS - 1 else nc.scalar.copy
+        for c in range(CHUNKS):
+            early_copy = nc.vector.tensor_copy if c == CHUNKS - 2 else nc.scalar.copy
             early_copy(out=h_grouped[c][:, :, 0:3], in_=h_sums[:, :, spans[c]].rearrange("p t s -> p s t"))
 
         def gather_add(t, c):

@@ -17,6 +17,7 @@ P = 128
 PACK = 4
 CHUNK = 128
 CHUNKS = S // CHUNK
+HALF = S // 2
 DMA_ALIGN = 256
 
 
@@ -59,7 +60,6 @@ def tile_picked_posadd_none_l_kernel(tc, xT, w1, w2, pe, offs, out):
             nc.sync.dma_start(out=pe_rows[t][:], in_=pe_dram[:, t, :])
         nc.sync.dma_start(out=w2_raw[:], in_=w2.rearrange("(p j) c -> p j c", j=PACK))
 
-        HALF = S // 2
         x_grouped = keep.tile([P, S, PACK], BF16, name="x_grouped", align_bytes=64)
         x_picked = [keep.tile([P, 2, HALF], F32, name="x_picked%d" % g) for g in range(2)]
         halves = [offsets[:, g * HALF // 16 : (g + 1) * HALF // 16] for g in range(2)]
@@ -99,41 +99,58 @@ def tile_picked_posadd_none_l_kernel(tc, xT, w1, w2, pe, offs, out):
 
         spans = [slice(c * CHUNK, (c + 1) * CHUNK) for c in range(CHUNKS)]
         lists = [offsets[:, c * CHUNK // 16 : (c + 1) * CHUNK // 16] for c in range(CHUNKS)]
-        h_grouped = [keep.tile([P, CHUNK, PACK], BF16, name="h_grouped%d" % c, align_bytes=64) for c in range(CHUNKS)]
+        h_all = keep.tile([P, S, PACK], BF16, name="h_all", align_bytes=64)
+        h_grouped = [h_all[:, spans[c], :] for c in range(CHUNKS)]
         h_sums = keep.tile([P, 3, S], F32, name="h_sums")
         nc.vector.tensor_copy(products[0][:], pe_rows[0][:].indirect(offsets[:]))
         nc.vector.tensor_tensor(h_sums[:, 0, :], banks[0][:], products[0][:], ADD)
         nc.vector.tensor_tensor(h_sums[:, 1, :], pe_rows[1][:].indirect(offsets[:]), products[1][:], ADD)
-        for c in range(CHUNKS):
+
+        for c in (2, 3, 0, 1):
             nc.vector.tensor_tensor(h_sums[:, 2, spans[c]], pe_rows[2][:].indirect(lists[c]), products[2][:, spans[c]], ADD)
-        for c in range(CHUNKS):
-            early_copy = nc.vector.tensor_copy if c == CHUNKS - 2 else nc.scalar.copy
+        for c in (2, 3, 0, 1):
+            early_copy = nc.vector.tensor_copy if c < 2 else nc.scalar.copy
             early_copy(out=h_grouped[c][:, :, 0:3], in_=h_sums[:, :, spans[c]].rearrange("p t s -> p s t"))
 
-        def gather_add(t, c):
-            plane = keep.tile([P, CHUNK], F32, name="h%d_%d" % (t, c))
-            nc.vector.tensor_tensor(plane[:], pe_rows[t][:].indirect(lists[c]), products[t][:, spans[c]], ADD)
-            return plane
-
+        last_plane = [keep.tile([P, CHUNK], F32, name="last_plane%d" % c) for c in range(CHUNKS)]
+        results = [keep.tile([P, CHUNK], F32, name="result%d" % c, align_bytes=DMA_ALIGN) for c in range(CHUNKS)]
         w2_grouped = keep.tile([P, N, PACK], BF16, name="w2_grouped", align_bytes=64)
-        pieces = [(c, 0, CHUNK) for c in range(CHUNKS - 1)] + [(CHUNKS - 1, 0, CHUNK // 2), (CHUNKS - 1, CHUNK // 2, CHUNK)]
-        last_plane = [gather_add(3, c) for c in range(CHUNKS)]
-        for c, lo, hi in pieces:
-            nc.scalar.copy(out=h_grouped[c][:, lo:hi, 3], in_=last_plane[c][:, lo:hi])
-        nc.vector.tensor_copy(out=w2_grouped[:], in_=w2_raw[:].rearrange("p j n -> p n j"))
+
+        def gather_add(c):
+            nc.vector.tensor_tensor(last_plane[c][:], pe_rows[3][:].indirect(lists[c]), products[3][:, spans[c]], ADD)
+
+        def round_last(copy, c, lo, hi):
+            copy(out=h_grouped[c][:, lo:hi, 3], in_=last_plane[c][:, lo:hi])
 
         def quantize_h(c, lo, hi):
-            return quantize("h%d_%d" % (c, lo), h_grouped[c][:, lo:hi, :].rearrange("p s j -> p (s j)"), hi - lo)
+            return (c, lo, hi), quantize("h%d_%d" % (c, lo), h_grouped[c][:, lo:hi, :].rearrange("p s j -> p (s j)"), hi - lo)
 
-        h_q = [quantize_h(*pieces[0])]
+        MID = CHUNK // 2
+        nc.scalar.copy(
+            out=w2_grouped[:].rearrange("p (c i) j -> p c j i", i=PACK),
+            in_=w2_raw[:].rearrange("p j (c i) -> p c j i", i=PACK),
+        )
+        gather_add(0)
+        gather_add(1)
+        round_last(nc.vector.tensor_copy, 0, 0, CHUNK)
+        gather_add(2)
+        gather_add(3)
+        round_last(nc.scalar.copy, 2, 0, CHUNK)
+        round_last(nc.scalar.copy, 3, 0, MID)
+        round_last(nc.scalar.copy, 3, MID, CHUNK)
+        h_q = [quantize_h(0, 0, CHUNK)]
         w2_codes, w2_scales = quantize("w2", w2_grouped[:].rearrange("p n j -> p (n j)"), N)
-        for piece in pieces[1:]:
+        round_last(nc.vector.tensor_copy, 1, 0, CHUNK)
+        pair = quantize("h_pair", h_all[:, CHUNK : 3 * CHUNK, :].rearrange("p s j -> p (s j)"), 2 * CHUNK)
+        for c in (1, 2):
+            cols = slice((c - 1) * CHUNK, c * CHUNK)
+            h_q.append(((c, 0, CHUNK), (pair[0][:, cols], pair[1][:, cols])))
+        for piece in ((3, 0, MID), (3, MID, CHUNK)):
             h_q.append(quantize_h(*piece))
-        results = [keep.tile([P, CHUNK], F32, name="result%d" % c, align_bytes=DMA_ALIGN) for c in range(CHUNKS)]
-        for i, (c, lo, hi) in enumerate(pieces):
+        for i, ((c, lo, hi), moving) in enumerate(h_q):
             bank = psum.tile([P, hi - lo], F32, name="out_bank%d" % i, tag="out_bank%d" % i if i < CHUNKS else "bank0")
-            multiply(bank[:], (w2_codes[:], w2_scales[:]), (h_q[i][0][:], h_q[i][1][:]))
+            multiply(bank[:], (w2_codes[:], w2_scales[:]), (moving[0][:], moving[1][:]))
             nc.scalar.copy(out=results[c][:, lo:hi], in_=bank[:])
             if hi == CHUNK:
-                queue = nc.scalar if c == CHUNKS - 1 else nc.sync
+                queue = nc.scalar if i == len(h_q) - 1 else nc.sync
                 queue.dma_start(out=out[:, spans[c]], in_=results[c][:])

@@ -112,45 +112,44 @@ def tile_picked_posadd_none_l_kernel(tc, xT, w1, w2, pe, offs, out):
             early_copy = nc.vector.tensor_copy if c < 2 else nc.scalar.copy
             early_copy(out=h_grouped[c][:, :, 0:3], in_=h_sums[:, :, spans[c]].rearrange("p t s -> p s t"))
 
-        last_plane = [keep.tile([P, CHUNK], F32, name="last_plane%d" % c) for c in range(CHUNKS)]
+        last_plane = keep.tile([P, S], F32, name="last_plane")
         results = [keep.tile([P, CHUNK], F32, name="result%d" % c, align_bytes=DMA_ALIGN) for c in range(CHUNKS)]
         w2_grouped = keep.tile([P, N, PACK], BF16, name="w2_grouped", align_bytes=64)
 
-        def gather_add(c):
-            nc.vector.tensor_tensor(last_plane[c][:], pe_rows[3][:].indirect(lists[c]), products[3][:, spans[c]], ADD)
+        def gather_add(lo, hi):
+            picked = pe_rows[3][:].indirect(offsets[:, lo // 16 : hi // 16])
+            nc.vector.tensor_tensor(last_plane[:, lo:hi], picked, products[3][:, lo:hi], ADD)
 
-        def round_last(copy, c, lo, hi):
-            copy(out=h_grouped[c][:, lo:hi, 3], in_=last_plane[c][:, lo:hi])
+        def round_last(copy, lo, hi):
+            copy(out=h_all[:, lo:hi, 3], in_=last_plane[:, lo:hi])
 
-        def quantize_h(c, lo, hi):
-            return (c, lo, hi), quantize("h%d_%d" % (c, lo), h_grouped[c][:, lo:hi, :].rearrange("p s j -> p (s j)"), hi - lo)
+        def quantize_h(lo, hi):
+            return (lo, hi), quantize("h%d" % lo, h_all[:, lo:hi, :].rearrange("p s j -> p (s j)"), hi - lo)
 
         MID = CHUNK // 2
+        THIRD_GATHER = 2 * CHUNK - 32
+        SCALAR_FROM = 2 * CHUNK - 16
         nc.scalar.copy(
             out=w2_grouped[:].rearrange("p (c i) j -> p c j i", i=PACK),
             in_=w2_raw[:].rearrange("p j (c i) -> p c j i", i=PACK),
         )
-        gather_add(0)
-        gather_add(1)
-        round_last(nc.vector.tensor_copy, 0, 0, CHUNK)
-        gather_add(2)
-        gather_add(3)
-        round_last(nc.scalar.copy, 2, 0, CHUNK)
-        round_last(nc.scalar.copy, 3, 0, MID)
-        round_last(nc.scalar.copy, 3, MID, CHUNK)
-        h_q = [quantize_h(0, 0, CHUNK)]
+        gather_add(0, CHUNK)
+        gather_add(CHUNK, THIRD_GATHER)
+        round_last(nc.vector.tensor_copy, 0, CHUNK)
+        gather_add(THIRD_GATHER, 3 * CHUNK)
+        gather_add(3 * CHUNK, S)
+        for lo, hi in ((SCALAR_FROM, 2 * CHUNK), (2 * CHUNK, 3 * CHUNK), (3 * CHUNK, S - MID), (S - MID, S)):
+            round_last(nc.scalar.copy, lo, hi)
+        round_last(nc.vector.tensor_copy, CHUNK, SCALAR_FROM)
+        h_q = [quantize_h(0, CHUNK)]
         w2_codes, w2_scales = quantize("w2", w2_grouped[:].rearrange("p n j -> p (n j)"), N)
-        round_last(nc.vector.tensor_copy, 1, 0, CHUNK)
-        pair = quantize("h_pair", h_all[:, CHUNK : 3 * CHUNK, :].rearrange("p s j -> p (s j)"), 2 * CHUNK)
-        for c in (1, 2):
-            cols = slice((c - 1) * CHUNK, c * CHUNK)
-            h_q.append(((c, 0, CHUNK), (pair[0][:, cols], pair[1][:, cols])))
-        for piece in ((3, 0, MID), (3, MID, CHUNK)):
-            h_q.append(quantize_h(*piece))
-        for i, ((c, lo, hi), moving) in enumerate(h_q):
+        for lo, hi in ((CHUNK, 2 * CHUNK), (2 * CHUNK, 3 * CHUNK), (3 * CHUNK, S - MID), (S - MID, S)):
+            h_q.append(quantize_h(lo, hi))
+        for i, ((lo, hi), moving) in enumerate(h_q):
+            c = lo // CHUNK
             bank = psum.tile([P, hi - lo], F32, name="out_bank%d" % i, tag="out_bank%d" % i if i < CHUNKS else "bank0")
             multiply(bank[:], (w2_codes[:], w2_scales[:]), (moving[0][:], moving[1][:]))
-            nc.scalar.copy(out=results[c][:, lo:hi], in_=bank[:])
-            if hi == CHUNK:
-                queue = nc.scalar if i == len(h_q) - 1 else nc.sync
+            nc.scalar.copy(out=results[c][:, lo - c * CHUNK : hi - c * CHUNK], in_=bank[:])
+            if hi % CHUNK == 0:
+                queue = nc.scalar if hi == S else nc.sync
                 queue.dma_start(out=out[:, spans[c]], in_=results[c][:])

@@ -12,6 +12,7 @@ U16 = mybir.dt.uint16
 U8 = mybir.dt.uint8
 FP8X4 = mybir.dt.float8_e4m3fn_x4
 ADD = mybir.AluOpType.add
+COPY = mybir.ActivationFunctionType.Copy
 
 P = 128
 PACK = 4
@@ -95,7 +96,8 @@ def tile_picked_posadd_none_l_kernel(tc, xT, w1, w2, pe, offs, out):
                     )
         products = [keep.tile([P, S], F32, name="product%d" % t) for t in range(PACK)]
         for t in range(1, PACK):
-            nc.scalar.copy(out=products[t][:], in_=banks[t][:])
+            width = HALF if t == 3 else S
+            nc.scalar.copy(out=products[t][:, :width], in_=banks[t][:, :width])
 
         spans = [slice(c * CHUNK, (c + 1) * CHUNK) for c in range(CHUNKS)]
         lists = [offsets[:, c * CHUNK // 16 : (c + 1) * CHUNK // 16] for c in range(CHUNKS)]
@@ -127,21 +129,28 @@ def tile_picked_posadd_none_l_kernel(tc, xT, w1, w2, pe, offs, out):
             return (lo, hi), quantize("h%d" % lo, h_all[:, lo:hi, :].rearrange("p s j -> p (s j)"), hi - lo)
 
         MID = CHUNK // 2
-        THIRD_GATHER = 2 * CHUNK - 32
-        SCALAR_FROM = 2 * CHUNK - 16
+        SHARE = 32
+        pe_picked = keep.tile([P, HALF], F32, name="pe_picked")
+        for c in (2, 3):
+            nc.scalar.activation(pe_picked[:, (c - 2) * CHUNK : (c - 1) * CHUNK], pe_rows[3][:].indirect(lists[c]), COPY)
         nc.scalar.copy(
             out=w2_grouped[:].rearrange("p (c i) j -> p c j i", i=PACK),
             in_=w2_raw[:].rearrange("p j (c i) -> p c j i", i=PACK),
         )
+
+        def add(c):
+            nc.vector.tensor_tensor(last_plane[:, spans[c]], banks[3][:, spans[c]], pe_picked[:, (c - 2) * CHUNK : (c - 1) * CHUNK], ADD)
+
         gather_add(0, CHUNK)
-        gather_add(CHUNK, THIRD_GATHER)
+        gather_add(CHUNK, HALF)
+        add(2)
         round_last(nc.vector.tensor_copy, 0, CHUNK)
-        gather_add(THIRD_GATHER, 3 * CHUNK)
-        gather_add(3 * CHUNK, S)
-        for lo, hi in ((SCALAR_FROM, 2 * CHUNK), (2 * CHUNK, 3 * CHUNK), (3 * CHUNK, S - MID), (S - MID, S)):
-            round_last(nc.scalar.copy, lo, hi)
-        round_last(nc.vector.tensor_copy, CHUNK, SCALAR_FROM)
+        add(3)
         h_q = [quantize_h(0, CHUNK)]
+        for lo, hi in ((CHUNK, HALF - SHARE), (HALF + SHARE, 3 * CHUNK)):
+            round_last(nc.vector.tensor_copy, lo, hi)
+        for lo, hi in ((HALF - SHARE, HALF + SHARE), (3 * CHUNK, S - MID), (S - MID, S)):
+            round_last(nc.scalar.copy, lo, hi)
         w2_codes, w2_scales = quantize("w2", w2_grouped[:].rearrange("p n j -> p (n j)"), N)
         for lo, hi in ((CHUNK, 2 * CHUNK), (2 * CHUNK, 3 * CHUNK), (3 * CHUNK, S - MID), (S - MID, S)):
             h_q.append(quantize_h(lo, hi))

@@ -96,8 +96,8 @@ def tile_picked_posadd_none_l_kernel(tc, xT, w1, w2, pe, offs, out):
                     )
         products = [keep.tile([P, S], F32, name="product%d" % t) for t in range(PACK)]
         for t in range(1, PACK):
-            width = HALF if t == 3 else S
-            nc.scalar.copy(out=products[t][:, :width], in_=banks[t][:, :width])
+            cols = (slice(0, S), slice(CHUNK, S), slice(0, HALF))[t - 1]
+            nc.scalar.copy(out=products[t][:, cols], in_=banks[t][:, cols])
 
         spans = [slice(c * CHUNK, (c + 1) * CHUNK) for c in range(CHUNKS)]
         lists = [offsets[:, c * CHUNK // 16 : (c + 1) * CHUNK // 16] for c in range(CHUNKS)]
@@ -108,8 +108,10 @@ def tile_picked_posadd_none_l_kernel(tc, xT, w1, w2, pe, offs, out):
         nc.vector.tensor_tensor(h_sums[:, 0, :], banks[0][:], products[0][:], ADD)
         nc.vector.tensor_tensor(h_sums[:, 1, :], pe_rows[1][:].indirect(offsets[:]), products[1][:], ADD)
 
-        for c in (2, 3, 0, 1):
+        nc.scalar.activation(products[2][:, spans[0]], pe_rows[2][:].indirect(lists[0]), COPY)
+        for c in (2, 3, 1):
             nc.vector.tensor_tensor(h_sums[:, 2, spans[c]], pe_rows[2][:].indirect(lists[c]), products[2][:, spans[c]], ADD)
+        nc.vector.tensor_tensor(h_sums[:, 2, spans[0]], banks[2][:, spans[0]], products[2][:, spans[0]], ADD)
         for c in (2, 3, 0, 1):
             early_copy = nc.vector.tensor_copy if c < 2 else nc.scalar.copy
             early_copy(out=h_grouped[c][:, :, 0:3], in_=h_sums[:, :, spans[c]].rearrange("p t s -> p s t"))

@@ -58,7 +58,8 @@ def tile_picked_posadd_none_l_kernel(tc, xT, w1, w2, pe, offs, out):
         nc.sync.dma_start(out=w1_raw[:], in_=w1.rearrange("(p j) c -> p j c", j=PACK))
         nc.sync.dma_start(out=x_late[:], in_=x_dram[:, 3, :])
         for t in range(PACK):
-            nc.sync.dma_start(out=pe_rows[t][:], in_=pe_dram[:, t, :])
+            for lo, hi in ((0, T // 2), (T // 2, T)) if t < 2 else ((0, T),):
+                nc.sync.dma_start(out=pe_rows[t][:, lo:hi], in_=pe_dram[:, t, lo:hi])
         nc.sync.dma_start(out=w2_raw[:], in_=w2.rearrange("(p j) c -> p j c", j=PACK))
 
         x_grouped = keep.tile([P, S, PACK], BF16, name="x_grouped", align_bytes=64)

@@ -12,6 +12,7 @@ U16 = mybir.dt.uint16
 U8 = mybir.dt.uint8
 FP8X4 = mybir.dt.float8_e4m3fn_x4
 ADD = mybir.AluOpType.add
+MULT = mybir.AluOpType.mult
 COPY = mybir.ActivationFunctionType.Copy
 
 P = 128
@@ -28,10 +29,11 @@ def tile_picked_posadd_none_l_kernel(tc, xT, w1, w2, pe, offs, out):
         keep = ctx.enter_context(tc.tile_pool(name="keep", bufs=1))
         psum = ctx.enter_context(tc.psum_pool(name="psum", bufs=1))
 
-        def quantize(name, grouped, width):
-            codes = keep.tile([P, width], U32, name=name + "_codes", align_bytes=64)
-            scales = keep.tile([P, width], U8, name=name + "_scales", align_bytes=64)
-            nc.vector.quantize_mx(out=codes[:].bitcast(FP8X4), scales=scales[:], in_=grouped)
+        def quantize(name, grouped, width, codes=None):
+            if codes is None:
+                codes = keep.tile([P, width], U32, name=name + "_codes", align_bytes=64)[:]
+            scales = keep.tile([P, width], U8, name=name + "_scales", align_bytes=64)[:]
+            nc.vector.quantize_mx(out=codes.bitcast(FP8X4), scales=scales, in_=grouped)
             return codes, scales
 
         def multiply(bank, stationary, moving):
@@ -46,6 +48,10 @@ def tile_picked_posadd_none_l_kernel(tc, xT, w1, w2, pe, offs, out):
             )
 
         offsets = keep.tile([P, S // 16], U16, name="offsets")
+
+        def entries(lo, hi):
+            return offsets[:, lo // 16 : hi // 16]
+
         w1_raw = keep.tile([P, PACK, H], F32, name="w1_raw", align_bytes=DMA_ALIGN)
         w2_raw = keep.tile([P, PACK, N], F32, name="w2_raw", align_bytes=DMA_ALIGN)
         x_early = keep.tile([P, 3, T], F32, name="x_early", align_bytes=DMA_ALIGN)
@@ -58,13 +64,13 @@ def tile_picked_posadd_none_l_kernel(tc, xT, w1, w2, pe, offs, out):
         nc.sync.dma_start(out=w1_raw[:], in_=w1.rearrange("(p j) c -> p j c", j=PACK))
         nc.sync.dma_start(out=x_late[:], in_=x_dram[:, 3, :])
         for t in range(PACK):
-            for lo, hi in ((0, T // 2), (T // 2, T)) if t < 2 else ((0, T),):
-                nc.sync.dma_start(out=pe_rows[t][:, lo:hi], in_=pe_dram[:, t, lo:hi])
+            for rows in (slice(0, P, 2), slice(1, P, 2)) if t < 2 else (slice(0, P),):
+                nc.sync.dma_start(out=pe_rows[t][rows, :], in_=pe_dram[rows, t, :])
         nc.sync.dma_start(out=w2_raw[:], in_=w2.rearrange("(p j) c -> p j c", j=PACK))
 
         x_grouped = keep.tile([P, S, PACK], BF16, name="x_grouped", align_bytes=64)
         x_picked = [keep.tile([P, 2, HALF], F32, name="x_picked%d" % g) for g in range(2)]
-        halves = [offsets[:, g * HALF // 16 : (g + 1) * HALF // 16] for g in range(2)]
+        halves = [entries(g * HALF, (g + 1) * HALF) for g in range(2)]
         for g in range(2):
             for t in range(2):
                 nc.vector.tensor_copy(x_picked[g][:, t, :], x_early[:, t, :].indirect(halves[g]))
@@ -90,20 +96,15 @@ def tile_picked_posadd_none_l_kernel(tc, xT, w1, w2, pe, offs, out):
             for g in range(2):
                 for t in planes:
                     cols = slice(t * P, (t + 1) * P)
-                    multiply(
-                        banks[t][:, g * HALF : (g + 1) * HALF],
-                        (w1_codes[:, cols], w1_scales[:, cols]),
-                        (x_q[g][0][:], x_q[g][1][:]),
-                    )
+                    multiply(banks[t][:, g * HALF : (g + 1) * HALF], (w1_codes[:, cols], w1_scales[:, cols]), x_q[g])
         products = [keep.tile([P, S], F32, name="product%d" % t) for t in range(PACK)]
         for t in range(1, PACK):
             cols = (slice(0, S), slice(CHUNK, S), slice(0, HALF))[t - 1]
             nc.scalar.copy(out=products[t][:, cols], in_=banks[t][:, cols])
 
         spans = [slice(c * CHUNK, (c + 1) * CHUNK) for c in range(CHUNKS)]
-        lists = [offsets[:, c * CHUNK // 16 : (c + 1) * CHUNK // 16] for c in range(CHUNKS)]
+        lists = [entries(c * CHUNK, (c + 1) * CHUNK) for c in range(CHUNKS)]
         h_all = keep.tile([P, S, PACK], BF16, name="h_all", align_bytes=64)
-        h_grouped = [h_all[:, spans[c], :] for c in range(CHUNKS)]
         h_sums = keep.tile([P, 3, S], F32, name="h_sums")
         nc.vector.tensor_copy(products[0][:], pe_rows[0][:].indirect(offsets[:]))
         nc.vector.tensor_tensor(h_sums[:, 0, :], banks[0][:], products[0][:], ADD)
@@ -115,53 +116,60 @@ def tile_picked_posadd_none_l_kernel(tc, xT, w1, w2, pe, offs, out):
         nc.vector.tensor_tensor(h_sums[:, 2, spans[0]], banks[2][:, spans[0]], products[2][:, spans[0]], ADD)
         for c in (2, 3, 0, 1):
             early_copy = nc.vector.tensor_copy if c < 2 else nc.scalar.copy
-            early_copy(out=h_grouped[c][:, :, 0:3], in_=h_sums[:, :, spans[c]].rearrange("p t s -> p s t"))
+            early_copy(out=h_all[:, spans[c], 0:3], in_=h_sums[:, :, spans[c]].rearrange("p t s -> p s t"))
 
         last_plane = keep.tile([P, S], F32, name="last_plane")
+        pe_picked = keep.tile([P, S], F32, name="pe_picked")
         results = [keep.tile([P, CHUNK], F32, name="result%d" % c, align_bytes=DMA_ALIGN) for c in range(CHUNKS)]
         w2_grouped = keep.tile([P, N, PACK], BF16, name="w2_grouped", align_bytes=64)
 
         def gather_add(lo, hi):
-            picked = pe_rows[3][:].indirect(offsets[:, lo // 16 : hi // 16])
-            nc.vector.tensor_tensor(last_plane[:, lo:hi], picked, products[3][:, lo:hi], ADD)
+            nc.vector.tensor_tensor(last_plane[:, lo:hi], pe_rows[3][:].indirect(entries(lo, hi)), products[3][:, lo:hi], ADD)
+
+        def gather(lo, hi):
+            nc.scalar.activation(pe_picked[:, lo:hi], pe_rows[3][:].indirect(entries(lo, hi)), COPY)
+
+        def add(lo, hi):
+            nc.vector.tensor_tensor(last_plane[:, lo:hi], banks[3][:, lo:hi], pe_picked[:, lo:hi], ADD)
+
+        def add_round(lo, hi):
+            nc.vector.tensor_tensor(h_all[:, lo:hi, 3], banks[3][:, lo:hi], pe_picked[:, lo:hi], ADD)
 
         def round_last(copy, lo, hi):
             copy(out=h_all[:, lo:hi, 3], in_=last_plane[:, lo:hi])
 
-        def quantize_h(lo, hi):
-            return (lo, hi), quantize("h%d" % lo, h_all[:, lo:hi, :].rearrange("p s j -> p (s j)"), hi - lo)
+        def quantize_h(lo, hi, codes=None):
+            return (lo, hi), quantize("h%d" % lo, h_all[:, lo:hi, :].rearrange("p s j -> p (s j)"), hi - lo, codes)
 
         MID = CHUNK // 2
         SHARE = 32
-        pe_picked = keep.tile([P, HALF], F32, name="pe_picked")
-        for c in (2, 3):
-            nc.scalar.activation(pe_picked[:, (c - 2) * CHUNK : (c - 1) * CHUNK], pe_rows[3][:].indirect(lists[c]), COPY)
+        gather(2 * CHUNK, 3 * CHUNK)
+        gather(3 * CHUNK, S)
         nc.scalar.copy(
             out=w2_grouped[:].rearrange("p (c i) j -> p c j i", i=PACK),
             in_=w2_raw[:].rearrange("p j (c i) -> p c j i", i=PACK),
         )
-
-        def add(c):
-            nc.vector.tensor_tensor(last_plane[:, spans[c]], banks[3][:, spans[c]], pe_picked[:, (c - 2) * CHUNK : (c - 1) * CHUNK], ADD)
-
         gather_add(0, CHUNK)
         gather_add(CHUNK, HALF)
-        add(2)
+        add(2 * CHUNK, 3 * CHUNK)
         round_last(nc.vector.tensor_copy, 0, CHUNK)
-        add(3)
+        add(3 * CHUNK, S)
         h_q = [quantize_h(0, CHUNK)]
         for lo, hi in ((CHUNK, HALF - SHARE), (HALF + SHARE, 3 * CHUNK)):
             round_last(nc.vector.tensor_copy, lo, hi)
         for lo, hi in ((HALF - SHARE, HALF + SHARE), (3 * CHUNK, S - MID), (S - MID, S)):
             round_last(nc.scalar.copy, lo, hi)
-        w2_codes, w2_scales = quantize("w2", w2_grouped[:].rearrange("p n j -> p (n j)"), N)
+        w2_q = quantize("w2", w2_grouped[:].rearrange("p n j -> p (n j)"), N)
         for lo, hi in ((CHUNK, 2 * CHUNK), (2 * CHUNK, 3 * CHUNK), (3 * CHUNK, S - MID), (S - MID, S)):
             h_q.append(quantize_h(lo, hi))
+
+        done = set()
         for i, ((lo, hi), moving) in enumerate(h_q):
             c = lo // CHUNK
             bank = psum.tile([P, hi - lo], F32, name="out_bank%d" % i, tag="out_bank%d" % i if i < CHUNKS else "bank0")
-            multiply(bank[:], (w2_codes[:], w2_scales[:]), (moving[0][:], moving[1][:]))
+            multiply(bank[:], w2_q, moving)
             nc.scalar.copy(out=results[c][:, lo - c * CHUNK : hi - c * CHUNK], in_=bank[:])
-            if hi % CHUNK == 0:
-                queue = nc.scalar if hi == S else nc.sync
+            done.add(lo)
+            if hi - lo == CHUNK or (lo ^ (CHUNK // 2)) in done:
+                queue = nc.scalar if i == len(h_q) - 1 else nc.sync
                 queue.dma_start(out=out[:, spans[c]], in_=results[c][:])

@@ -64,7 +64,7 @@ def tile_picked_posadd_none_l_kernel(tc, xT, w1, w2, pe, offs, out):
         nc.sync.dma_start(out=w1_raw[:], in_=w1.rearrange("(p j) c -> p j c", j=PACK))
         nc.sync.dma_start(out=x_late[:], in_=x_dram[:, 3, :])
         for t in range(PACK):
-            for rows in (slice(0, P, 2), slice(1, P, 2)) if t < 2 else (slice(0, P),):
+            for rows in (slice(0, P, 2), slice(1, P, 2)) if t < 3 else (slice(0, P),):
                 nc.sync.dma_start(out=pe_rows[t][rows, :], in_=pe_dram[rows, t, :])
         nc.sync.dma_start(out=w2_raw[:], in_=w2.rearrange("(p j) c -> p j c", j=PACK))
 

@@ -171,5 +171,4 @@ def tile_picked_posadd_none_l_kernel(tc, xT, w1, w2, pe, offs, out):
             nc.scalar.copy(out=results[c][:, lo - c * CHUNK : hi - c * CHUNK], in_=bank[:])
             done.add(lo)
             if hi - lo == CHUNK or (lo ^ (CHUNK // 2)) in done:
-                queue = nc.scalar if i == len(h_q) - 1 else nc.sync
-                queue.dma_start(out=out[:, spans[c]], in_=results[c][:])
+                nc.sync.dma_start(out=out[:, spans[c]], in_=results[c][:])

from contextlib import ExitStack

import concourse.mybir as mybir

K, T, S, H, N = 512, 2048, 512, 512, 128
FLOPS = 2 * K * H * S + 2 * H * N * S

F32 = mybir.dt.float32
BF16 = mybir.dt.bfloat16
U32 = mybir.dt.uint32
U16 = mybir.dt.uint16
U8 = mybir.dt.uint8
FP8X4 = mybir.dt.float8_e4m3fn_x4
ADD = mybir.AluOpType.add
MULT = mybir.AluOpType.mult
COPY = mybir.ActivationFunctionType.Copy

P = 128
PACK = 4
CHUNK = 128
CHUNKS = S // CHUNK
HALF = S // 2
DMA_ALIGN = 256


def tile_picked_posadd_none_l_kernel(tc, xT, w1, w2, pe, offs, out):
    nc = tc.nc
    with ExitStack() as ctx:
        keep = ctx.enter_context(tc.tile_pool(name="keep", bufs=1))
        psum = ctx.enter_context(tc.psum_pool(name="psum", bufs=1))

        def quantize(name, grouped, width, codes=None):
            if codes is None:
                codes = keep.tile([P, width], U32, name=name + "_codes", align_bytes=64)[:]
            scales = keep.tile([P, width], U8, name=name + "_scales", align_bytes=64)[:]
            nc.vector.quantize_mx(out=codes.bitcast(FP8X4), scales=scales, in_=grouped)
            return codes, scales

        def multiply(bank, stationary, moving):
            nc.tensor.matmul_mx(
                out=bank,
                lhsT=stationary[0].bitcast(FP8X4),
                lhsT_scale=stationary[1],
                rhs=moving[0].bitcast(FP8X4),
                rhs_scale=moving[1],
                start=True,
                stop=True,
            )

        offsets = keep.tile([P, S // 16], U16, name="offsets")

        def entries(lo, hi):
            return offsets[:, lo // 16 : hi // 16]

        w1_raw = keep.tile([P, PACK, H], F32, name="w1_raw", align_bytes=DMA_ALIGN)
        w2_raw = keep.tile([P, PACK, N], F32, name="w2_raw", align_bytes=DMA_ALIGN)
        x_early = keep.tile([P, 3, T], F32, name="x_early", align_bytes=DMA_ALIGN)
        x_late = keep.tile([P, T], F32, name="x_late", align_bytes=DMA_ALIGN)
        pe_rows = [keep.tile([P, T], F32, name="pe_rows%d" % t, align_bytes=DMA_ALIGN) for t in range(PACK)]
        x_dram = xT.rearrange("(p j) w -> p j w", j=PACK)
        pe_dram = pe.rearrange("(p j) w -> p j w", j=PACK)
        nc.sync.dma_start(out=x_early[:], in_=x_dram[:, 0:3, :])
        nc.sync.dma_start(offsets[:], offs)
        nc.sync.dma_start(out=w1_raw[:], in_=w1.rearrange("(p j) c -> p j c", j=PACK))
        nc.sync.dma_start(out=x_late[:], in_=x_dram[:, 3, :])
        for t in range(PACK):
            for rows in (slice(0, P, 2), slice(1, P, 2)) if t < 3 else (slice(0, P),):
                nc.sync.dma_start(out=pe_rows[t][rows, :], in_=pe_dram[rows, t, :])
        nc.sync.dma_start(out=w2_raw[:], in_=w2.rearrange("(p j) c -> p j c", j=PACK))

        x_grouped = keep.tile([P, S, PACK], BF16, name="x_grouped", align_bytes=64)
        x_picked = [keep.tile([P, 2, HALF], F32, name="x_picked%d" % g) for g in range(2)]
        halves = [entries(g * HALF, (g + 1) * HALF) for g in range(2)]
        for g in range(2):
            for t in range(2):
                nc.vector.tensor_copy(x_picked[g][:, t, :], x_early[:, t, :].indirect(halves[g]))
        nc.vector.tensor_copy(x_grouped[:, :, 2], x_early[:, 2, :].indirect(offsets[:]))
        for g in range(2):
            nc.vector.tensor_copy(x_grouped[:, g * HALF : (g + 1) * HALF, 3], x_late[:].indirect(halves[g]))
        nc.scalar.copy(out=x_grouped[:, :HALF, 0:2], in_=x_picked[0][:].rearrange("p t s -> p s t"))

        w1_grouped = keep.tile([P, H * PACK], BF16, name="w1_grouped", align_bytes=64)
        nc.scalar.copy(
            out=w1_grouped[:].rearrange("p (t m j) -> p m t j", t=PACK, j=PACK),
            in_=w1_raw[:].rearrange("p j (m t) -> p m t j", t=PACK),
        )
        nc.scalar.copy(out=x_grouped[:, HALF:, 0:2], in_=x_picked[1][:].rearrange("p t s -> p s t"))
        w1_codes, w1_scales = quantize("w1", w1_grouped[:], H)
        x_q = [
            quantize("x%d" % g, x_grouped[:, g * HALF : (g + 1) * HALF, :].rearrange("p s j -> p (s j)"), HALF)
            for g in range(2)
        ]

        banks = [psum.tile([P, S], F32, name="bank%d" % t) for t in range(PACK)]
        for planes in ((1, 0), (2, 3)):
            for g in range(2):
                for t in planes:
                    cols = slice(t * P, (t + 1) * P)
                    multiply(banks[t][:, g * HALF : (g + 1) * HALF], (w1_codes[:, cols], w1_scales[:, cols]), x_q[g])
        products = [keep.tile([P, S], F32, name="product%d" % t) for t in range(PACK)]
        for t in range(1, PACK):
            cols = (slice(0, S), slice(CHUNK, S), slice(0, HALF))[t - 1]
            nc.scalar.copy(out=products[t][:, cols], in_=banks[t][:, cols])

        spans = [slice(c * CHUNK, (c + 1) * CHUNK) for c in range(CHUNKS)]
        lists = [entries(c * CHUNK, (c + 1) * CHUNK) for c in range(CHUNKS)]
        h_all = keep.tile([P, S, PACK], BF16, name="h_all", align_bytes=64)
        h_sums = keep.tile([P, 3, S], F32, name="h_sums")
        nc.vector.tensor_copy(products[0][:], pe_rows[0][:].indirect(offsets[:]))
        nc.vector.tensor_tensor(h_sums[:, 0, :], banks[0][:], products[0][:], ADD)
        nc.vector.tensor_tensor(h_sums[:, 1, :], pe_rows[1][:].indirect(offsets[:]), products[1][:], ADD)

        nc.scalar.activation(products[2][:, spans[0]], pe_rows[2][:].indirect(lists[0]), COPY)
        for c in (2, 3, 1):
            nc.vector.tensor_tensor(h_sums[:, 2, spans[c]], pe_rows[2][:].indirect(lists[c]), products[2][:, spans[c]], ADD)
        nc.vector.tensor_tensor(h_sums[:, 2, spans[0]], banks[2][:, spans[0]], products[2][:, spans[0]], ADD)
        for c in (2, 3, 0, 1):
            early_copy = nc.vector.tensor_copy if c < 2 else nc.scalar.copy
            early_copy(out=h_all[:, spans[c], 0:3], in_=h_sums[:, :, spans[c]].rearrange("p t s -> p s t"))

        last_plane = keep.tile([P, S], F32, name="last_plane")
        pe_picked = keep.tile([P, S], F32, name="pe_picked")
        results = [keep.tile([P, CHUNK], F32, name="result%d" % c, align_bytes=DMA_ALIGN) for c in range(CHUNKS)]
        w2_grouped = keep.tile([P, N, PACK], BF16, name="w2_grouped", align_bytes=64)

        def gather_add(lo, hi):
            nc.vector.tensor_tensor(last_plane[:, lo:hi], pe_rows[3][:].indirect(entries(lo, hi)), products[3][:, lo:hi], ADD)

        def gather(lo, hi):
            nc.scalar.activation(pe_picked[:, lo:hi], pe_rows[3][:].indirect(entries(lo, hi)), COPY)

        def add(lo, hi):
            nc.vector.tensor_tensor(last_plane[:, lo:hi], banks[3][:, lo:hi], pe_picked[:, lo:hi], ADD)

        def add_round(lo, hi):
            nc.vector.tensor_tensor(h_all[:, lo:hi, 3], banks[3][:, lo:hi], pe_picked[:, lo:hi], ADD)

        def round_last(copy, lo, hi):
            copy(out=h_all[:, lo:hi, 3], in_=last_plane[:, lo:hi])

        def quantize_h(lo, hi, codes=None):
            return (lo, hi), quantize("h%d" % lo, h_all[:, lo:hi, :].rearrange("p s j -> p (s j)"), hi - lo, codes)

        MID = CHUNK // 2
        SHARE = 32
        gather(2 * CHUNK, 3 * CHUNK)
        gather(3 * CHUNK, S)
        nc.scalar.copy(
            out=w2_grouped[:].rearrange("p (c i) j -> p c j i", i=PACK),
            in_=w2_raw[:].rearrange("p j (c i) -> p c j i", i=PACK),
        )
        gather_add(0, CHUNK)
        gather_add(CHUNK, HALF)
        add(2 * CHUNK, 3 * CHUNK)
        round_last(nc.vector.tensor_copy, 0, CHUNK)
        add(3 * CHUNK, S)
        h_q = [quantize_h(0, CHUNK)]
        for lo, hi in ((CHUNK, HALF - SHARE), (HALF + SHARE, 3 * CHUNK)):
            round_last(nc.vector.tensor_copy, lo, hi)
        for lo, hi in ((HALF - SHARE, HALF + SHARE), (3 * CHUNK, S - MID), (S - MID, S)):
            round_last(nc.scalar.copy, lo, hi)
        w2_q = quantize("w2", w2_grouped[:].rearrange("p n j -> p (n j)"), N)
        for lo, hi in ((CHUNK, 2 * CHUNK), (2 * CHUNK, 3 * CHUNK), (3 * CHUNK, S - MID), (S - MID, S)):
            h_q.append(quantize_h(lo, hi))

        done = set()
        for i, ((lo, hi), moving) in enumerate(h_q):
            c = lo // CHUNK
            bank = psum.tile([P, hi - lo], F32, name="out_bank%d" % i, tag="out_bank%d" % i if i < CHUNKS else "bank0")
            multiply(bank[:], w2_q, moving)
            nc.scalar.copy(out=results[c][:, lo - c * CHUNK : hi - c * CHUNK], in_=bank[:])
            done.add(lo)
            if hi - lo == CHUNK or (lo ^ (CHUNK // 2)) in done:
                nc.sync.dma_start(out=out[:, spans[c]], in_=results[c][:])
